import numpy as np
import ml_dtypes


def mxq(x, axis, fmt="e4m3"):
    dtype, down = {"e4m3": (ml_dtypes.float8_e4m3fn, 7), "e5m2": (ml_dtypes.float8_e5m2, 14)}[fmt]
    v = np.moveaxis(np.asarray(x, np.float32).astype(ml_dtypes.bfloat16).astype(np.float64), axis, -1)
    blocks = v.reshape(v.shape[:-1] + (-1, 32))
    amax = np.abs(blocks).max(-1, keepdims=True)
    byte = np.maximum(np.where(amax > 0, np.frexp(amax)[1] - 1 + 127, 0) - down, 1)
    scale = np.exp2(byte - 127.0)
    codes = (blocks / scale).astype(np.float32).astype(dtype).astype(np.float64)
    return np.moveaxis((codes * scale).reshape(v.shape), -1, axis)


WIDE = False


def mx_kscale(k):
    if not WIDE:
        return np.ones(k)
    levels = np.array([10, -10, 5, -5, 0])
    if k % 512:
        return np.exp2(np.random.permutation(np.resize(levels, k // 32))).repeat(32)
    a = np.empty((k // 512, 16))
    for p in range(k // 512):
        a[p, :8] = np.random.permutation(np.resize(levels, 8))
        for g in range(8):
            far = levels[np.abs(levels - a[p, g]) >= 10]
            a[p, g + 8] = far[np.random.randint(len(far))]
    return np.exp2(a.ravel()).repeat(32)


def f64(x):
    return np.asarray(x).astype(np.float64)


def striped(idx):
    return np.tile(idx.reshape(-1, 16).T, (8, 1)).astype(np.uint16)


def unstriped(offs):
    return offs[:16].T.reshape(-1).astype(np.int64)


E2M1 = np.array([0.0, 0.5, 1.0, 1.5, 2.0, 3.0, 4.0, 6.0, -0.0, -0.5, -1.0, -1.5, -2.0, -3.0, -4.0, -6.0])


def pack_weight(w, fmt):
    k, n = w.shape
    w = f64(np.asarray(w, np.float32).astype(ml_dtypes.bfloat16)).reshape(k // 32, 32, n)
    amax = np.abs(w).max(1)
    if fmt == "e4m3":
        byte = np.frexp(amax)[1] - 1 + 127 - 7
    else:
        mant, ex = np.frexp(amax / 6.0)
        byte = np.where(mant > 0.5, ex, ex - 1) + 127
    byte = np.clip(np.where(amax > 0, byte, 1), 1, 254)
    scaled = (w * np.exp2(127.0 - byte)[:, None, :]).reshape(k, n).astype(np.float32)
    by_word = np.ascontiguousarray(scaled.reshape(k // 512, 128, 4, n).transpose(0, 1, 3, 2))
    if fmt == "e4m3":
        words = by_word.astype(ml_dtypes.float8_e4m3fn).view(np.uint8)
    else:
        c = by_word.astype(ml_dtypes.float4_e2m1fn).view(np.uint8) & 0xF
        words = (c[..., 0::2] | (c[..., 1::2] << 4)).reshape(k // 512, 128, 2 * n)
    return np.ascontiguousarray(words), np.ascontiguousarray(byte.astype(np.uint8).reshape(k // 512, 16, n))


def unpack_weight(words, scales, fmt):
    g, _, n = scales.shape
    words = np.ascontiguousarray(words).reshape(g, 128, n, -1)
    if fmt == "e4m3":
        vals = words.view(ml_dtypes.float8_e4m3fn).astype(np.float64)
    else:
        nib = np.empty((g, 128, n, 4), np.uint8)
        nib[..., 0::2] = words & 0xF
        nib[..., 1::2] = words >> 4
        vals = E2M1[nib]
    vals = vals * np.repeat(np.exp2(scales.astype(np.float64) - 127.0), 8, axis=1)[..., None]
    return vals.transpose(0, 1, 3, 2).reshape(g * 512, n)


def gelu(v):
    return 0.5 * v * (1.0 + np.tanh(np.sqrt(2.0 / np.pi) * (v + 0.044715 * v**3)))


K, H, T, S, T3, S2, P = 1024, 512, 4096, 1024, 2048, 1024, 512


def setup_inputs():
    n = np.random.standard_normal
    s = mx_kscale(K)[:, None]
    u = mx_kscale(H)[:, None]
    tab_words, tab_scales = pack_weight(n((K, T)) * s, "e4m3")
    tab2_words, tab2_scales = pack_weight(n((H, T3)) / np.sqrt(H) / u, "e4m3")
    w2_words, w2_scales = pack_weight(0.5 * n((K, H)) / np.sqrt(K) / s * u.T, "e2m1")
    return {
        "tab_words": tab_words, "tab_scales": tab_scales,
        "offs": striped(np.random.permutation(T)[:S]),
        "tab2_words": tab2_words, "tab2_scales": tab2_scales,
        "offs2": striped(np.random.permutation(T3)[:S2]),
        "pos1": striped(np.random.permutation(S)[:P]),
        "pos2": striped(np.random.permutation(S)[:P]),
        "w1": (1.5 * n((K, H)) / np.sqrt(K) / s).astype(np.float32),
        "w2_words": w2_words, "w2_scales": w2_scales,
        "gain": (np.random.uniform(0.4, 1.0, H) * u[:, 0]).astype(np.float32),
        "w3": (n((H, S2)) / np.sqrt(H) / u).astype(np.float32),
        "steep": np.random.uniform(1, 3, S2).astype(np.float32),
        "share": np.random.uniform(0.1, 0.5, S2).astype(np.float32),
        "lat": (0.4 * n(S2)).astype(np.float32),
    }


def reference(tab_words, tab_scales, offs, tab2_words, tab2_scales, offs2, pos1, pos2,
              w1, w2_words, w2_scales, gain, w3, steep, share, lat):
    v = unpack_weight(tab_words, tab_scales, "e4m3")[:, unstriped(offs)]
    v2 = unpack_weight(tab2_words, tab2_scales, "e4m3")[:, unstriped(offs2)]
    w2 = unpack_weight(w2_words, w2_scales, "e2m1")
    f = mxq(f64(w1), 0, "e4m3").T @ v
    h = f64(gain)[:, None] * (f / (1.0 + np.exp(-f))) + (w2.T @ v)
    hq = mxq(h, 0, "e4m3")
    e = v2.T @ hq
    d = mxq(f64(w3), 0, "e4m3").T @ hq
    top = e.max(axis=1)
    a = 1.0 / (1.0 + np.exp(-f64(steep)[:, None] * (e[:, unstriped(pos1)] - f64(share)[:, None] * top[:, None])))
    c = d[:, unstriped(pos2)]
    return c * a + f64(lat)[:, None] * np.abs(c)

@@ -1,0 +1,305 @@
+from contextlib import ExitStack
+
+import concourse.mybir as mybir
+from concourse.masks import make_identity
+
+K, H, T, S, T3, S2, NP = 1024, 512, 4096, 1024, 2048, 1024, 512
+FLOPS = 2 * (2 * K * H * S + 2 * H * S2 * S)
+
+F32 = mybir.dt.float32
+BF16 = mybir.dt.bfloat16
+I32 = mybir.dt.int32
+U32 = mybir.dt.uint32
+U16 = mybir.dt.uint16
+U8 = mybir.dt.uint8
+FP8X4 = mybir.dt.float8_e4m3fn_x4
+FP4X4 = mybir.dt.float4_e2m1fn_x4
+ALU = mybir.AluOpType
+ACT = mybir.ActivationFunctionType
+
+P = 128
+PACK = 4
+BANK = 512
+PASSES = K // (P * PACK)
+HALVES = S // BANK
+ROW_TILES = S2 // P
+QUADS = 4
+W3_LOADS = 2
+W3_PIECE = 256
+
+
+def tile_list_salt_screen_scores_kernel(
+    tc, tab_words, tab_scales, offs, tab2_words, tab2_scales, offs2, pos1, pos2,
+    w1, w2_words, w2_scales, gain, w3, steep, share, lat, out,
+):
+    nc = tc.nc
+    with ExitStack() as ctx:
+        keep = ctx.enter_context(tc.tile_pool(name="keep", bufs=1))
+        ring = ctx.enter_context(tc.tile_pool(name="ring", bufs=3))
+        turns = ctx.enter_context(tc.tile_pool(name="turns", bufs=1))
+        psum = ctx.enter_context(tc.psum_pool(name="psum", bufs=1))
+
+        def held(name, shape, dtype):
+            return keep.tile(shape, dtype, name=name, align_bytes=64)
+
+        def tenant(name, shape, dtype, kib):
+            return turns.tile(shape, dtype, name=name, align_bytes=64, offset=kib * 1024)
+
+        def bank(name, number):
+            return psum.tile([P, BANK], F32, name=name, offset=number * BANK * 4)
+
+        idx = held("idx", [P, S // 16], U16)
+        idx2 = held("idx2", [P, S2 // 16], U16)
+        p1 = held("p1", [P, NP // 16], U16)
+        p2 = held("p2", [P, NP // 16], U16)
+
+        tab_s = tenant("tab_s", [P, T], U8, 52)
+        tab2_s = held("tab2_s", [P, T3], U8)
+        w2_s_raw = held("w2_s_raw", [P, PASSES * H], U8)
+        v_s1 = held("v_s1", [P, S], U8)
+        nc.vector.memset(tab_s[:].bitcast(I32), 0)
+        for plane in (w2_s_raw, tab2_s, v_s1):
+            nc.vector.memset(plane[:].bitcast(I32), 0)
+        ident = held("ident", [P, P], F32)
+        make_identity(nc, ident[:])
+
+        tab_w = [tenant("tab_w0", [P, T], I32, 0)]
+        w1_raw = [tenant("w1_raw%d" % a, [P, PACK, H], F32, 16 + 8 * a) for a in range(PASSES)]
+        w2_raw = held("w2_raw", [P, PASSES, H], U16)
+        w3_cols = S2 // W3_LOADS
+
+        def load_words(tile, words):
+            nc.sync.dma_start(out=tile[:], in_=words.rearrange("p t i -> p (t i)").bitcast(I32))
+
+        def load_w1(a):
+            nc.sync.dma_start(out=w1_raw[a][:], in_=w1[a * 512 : (a + 1) * 512, :].rearrange("(p j) c -> p j c", j=PACK))
+
+        for tile, source in ((idx, offs), (idx2, offs2), (p1, pos1), (p2, pos2)):
+            nc.sync.dma_start(out=tile[:], in_=source)
+        load_words(tab_w[0], tab_words[0])
+        nc.sync.dma_start(
+            out=w2_raw[:].rearrange("p a c -> p (a c)").bitcast(I32).rearrange("p (a c) -> p a c", a=PASSES),
+            in_=w2_words.bitcast(I32).rearrange("a p c -> p a c"),
+        )
+        load_w1(0)
+        load_w1(1)
+        for q in range(QUADS):
+            nc.scalar.dma_start(
+                out=tab_s[:].bitcast(I32)[32 * q : 32 * q + 8, :],
+                in_=tab_scales.bitcast(I32)[:, 4 * q : 4 * q + 4, :],
+            )
+        for q in range(QUADS):
+            nc.gpsimd.dma_start(
+                out=w2_s_raw[:].bitcast(I32)[32 * q : 32 * q + 4, :].rearrange("p (a c) -> p a c", a=PASSES),
+                in_=w2_scales.bitcast(I32)[:, 4 * q : 4 * q + 4, :].rearrange("a r c -> r a c"),
+            )
+
+        v_s = held("v_s", [P, S], U8)
+        nc.vector.tensor_copy(out=v_s[:], in_=tab_s[:].indirect(idx[:]))
+        nc.gpsimd.dma_start(out=v_s1[:].bitcast(I32)[0:100, :], in_=v_s[:].bitcast(I32)[4:104, :])
+        rows = tenant("rows", [P, P], F32, 52)
+        gain_t = tenant("gain_t", [P, PACK], F32, 53)
+        nc.vector.memset(rows[:], 0.0)
+        v_scale = [v_s, v_s1]
+        for q in range(QUADS):
+            nc.gpsimd.dma_start(
+                out=tab2_s[:].bitcast(I32)[32 * q : 32 * q + 4, :],
+                in_=tab2_scales.bitcast(I32)[0, 4 * q : 4 * q + 4, :],
+            )
+        nc.gpsimd.dma_start(out=gain_t[:], in_=gain.rearrange("(p t) -> p t", t=PACK))
+        for n, vec in enumerate((steep, share, lat)):
+            nc.gpsimd.dma_start(out=rows[ROW_TILES * n : ROW_TILES * (n + 1), :], in_=vec.rearrange("(i p) -> i p", p=P))
+
+        v_w = [[held("v_w%d_%d" % (a, hf), [P, BANK], U32) for hf in range(HALVES)] for a in range(PASSES)]
+
+        def gather_v(a, hf):
+            nc.vector.tensor_copy(
+                out=v_w[a][hf][:],
+                in_=tab_w[a][:].bitcast(U32).indirect(idx[:, hf * 32 : (hf + 1) * 32]),
+            )
+
+        for hf in range(HALVES):
+            gather_v(0, hf)
+        tab_w.append(tenant("tab_w1", [P, T], I32, 0))
+        load_words(tab_w[1], tab_words[1])
+
+        w2_w = held("w2_w", [P, PASSES, H], U16)
+        w2_s = held("w2_s", [P, PASSES * H], U8)
+        for a in range(PASSES):
+            nc.vector.tensor_copy(
+                out=w2_w[:, a, :].rearrange("p (t m) -> p t m", t=PACK),
+                in_=w2_raw[:, a, :].rearrange("p (m t) -> p t m", t=PACK),
+            )
+        nc.vector.tensor_copy(
+            out=w2_s[:].rearrange("p (a t m) -> p a t m", a=PASSES, t=PACK),
+            in_=w2_s_raw[:].rearrange("p (a m t) -> p a t m", a=PASSES, t=PACK),
+        )
+
+        v2_s = held("v2_s", [P, S2], U8)
+        nc.vector.tensor_copy(out=v2_s[:], in_=tab2_s[:].indirect(idx2[:]))
+
+        w1_w = [held("w1_w%d" % a, [P, H], U32) for a in range(PASSES)]
+        w1_s = [held("w1_s%d" % a, [P, H], U8) for a in range(PASSES)]
+        for a in range(PASSES):
+            w1_bf = tenant("w1_bf%d" % a, [P, H * PACK], BF16, 32 + 8 * a)
+            nc.scalar.copy(
+                out=w1_bf[:].rearrange("p (t m j) -> p m t j", t=PACK, j=PACK),
+                in_=w1_raw[a][:].rearrange("p j (m t) -> p m t j", t=PACK),
+            )
+            nc.vector.quantize_mx(out=w1_w[a][:].bitcast(FP8X4), scales=w1_s[a][:], in_=w1_bf[:])
+        tab2_w = tenant("tab2_w", [P, T3], I32, 16)
+        load_words(tab2_w, tab2_words[0])
+        w3_raw = []
+        for b in range(W3_LOADS):
+            w3_raw.append(tenant("w3_raw%d" % b, [P, PACK, w3_cols], F32, 32 - 8 * b))
+            nc.sync.dma_start(
+                out=w3_raw[b][:],
+                in_=w3[:, b * w3_cols : (b + 1) * w3_cols].rearrange("(p j) c -> p j c", j=PACK),
+            )
+
+        for hf in range(HALVES):
+            gather_v(1, hf)
+
+
+        h_w = [held("h_w%d" % hf, [P, BANK], U32) for hf in range(HALVES)]
+        h_s = [held("h_s%d" % hf, [P, BANK], U8) for hf in range(HALVES)]
+        v2_w = tenant("v2_w", [P, S2], U32, 0)
+
+        for hf in range(HALVES):
+            cs = slice(hf * BANK, (hf + 1) * BANK)
+            f_bank = [bank("f%d_%d" % (hf, t), t) for t in range(PACK)]
+            g_bank = [bank("g%d_%d" % (hf, t), PACK + t) for t in range(PACK)]
+            steps = [(a, t) for a in range(PASSES) for t in range(PACK)]
+            if hf > 0:
+                steps = sorted(steps, key=lambda step: (step[1], step[0]))
+            for a, t in steps:
+                if True:
+                    nc.tensor.matmul_mx(
+                        out=f_bank[t][:], lhsT=w1_w[a][:, t * P : (t + 1) * P].bitcast(FP8X4),
+                        lhsT_scale=w1_s[a][:, t * P : (t + 1) * P],
+                        rhs=v_w[a][hf][:].bitcast(FP8X4), rhs_scale=v_scale[a][:, cs],
+                        start=(a == 0), stop=(a == PASSES - 1),
+                    )
+                    nc.tensor.matmul_mx(
+                        out=g_bank[t][:], lhsT=w2_w[:, a, t * P : (t + 1) * P].bitcast(FP4X4),
+                        lhsT_scale=w2_s[:, a * H + t * P : a * H + (t + 1) * P],
+                        rhs=v_w[a][hf][:].bitcast(FP8X4), rhs_scale=v_scale[a][:, cs],
+                        start=(a == 0), stop=(a == PASSES - 1),
+                    )
+            h_planes = held("h_planes%d" % hf, [P, PACK, BANK], BF16)
+            for t in range(PACK):
+                bent = ring.tile([P, BANK], F32, name="bent")
+                nc.scalar.activation(out=bent[:], in_=f_bank[t][:], func=ACT.Silu)
+                nc.vector.scalar_tensor_tensor(
+                    out=h_planes[:, t, :], in0=bent[:], scalar=gain_t[:, t : t + 1], in1=g_bank[t][:],
+                    op0=ALU.mult, op1=ALU.add,
+                )
+            h_bf = tenant("h_bf%d" % hf, [P, BANK * PACK], BF16, 44 + 4 * hf)
+            nc.scalar.copy(
+                out=h_bf[:].rearrange("p (c i t) -> p c t i", i=4, t=PACK),
+                in_=h_planes[:].rearrange("p t (c i) -> p c t i", i=4),
+            )
+            nc.vector.quantize_mx(out=h_w[hf][:].bitcast(FP8X4), scales=h_s[hf][:], in_=h_bf[:])
+            nc.vector.tensor_copy(
+                out=v2_w[:, cs], in_=tab2_w[:].bitcast(U32).indirect(idx2[:, hf * 32 : (hf + 1) * 32]),
+            )
+
+        turned = bank("turned", 2)
+        nc.tensor.transpose(turned[:, :P], rows[:], ident[:])
+        cols = held("cols", [P, 3 * ROW_TILES], F32)
+        nc.scalar.copy(out=cols[:], in_=turned[:, : 3 * ROW_TILES])
+
+        shift = held("shift", [P, ROW_TILES], F32)
+        nc.vector.scalar_tensor_tensor(
+            out=shift[:], in0=cols[:, :ROW_TILES], scalar=-1.0, in1=cols[:, ROW_TILES : 2 * ROW_TILES],
+            op0=ALU.mult, op1=ALU.mult,
+        )
+        w3_w = tenant("w3_w", [P, S2], U32, 48)
+        w3_s = held("w3_s", [P, S2], U8)
+
+        def quantise_w3(piece):
+            c0 = piece * W3_PIECE
+            b, off = divmod(c0, w3_cols)
+            w3_bf = held("w3_bf%d" % piece, [P, W3_PIECE * PACK], BF16)
+            for part in range(W3_PIECE // P):
+                nc.gpsimd.tensor_scalar(
+                    out=w3_bf[:, part * P * PACK : (part + 1) * P * PACK].rearrange("p (c j) -> p c j", j=PACK),
+                    in0=w3_raw[b][:, :, off + part * P : off + (part + 1) * P].rearrange("p j c -> p c j"),
+                    scalar1=1.0, scalar2=0.0, op0=ALU.mult, op1=ALU.add,
+                )
+            nc.vector.quantize_mx(
+                out=w3_w[:, c0 : c0 + W3_PIECE].bitcast(FP8X4), scales=w3_s[:, c0 : c0 + W3_PIECE], in_=w3_bf[:],
+            )
+
+        tops = held("tops", [P, HALVES * ROW_TILES], F32)
+        bias = held("bias", [P, ROW_TILES], F32)
+        e_sb, d_sb, gate, picked, size, gated = {}, {}, {}, {}, {}, {}
+
+        def rows_of(i):
+            return slice(i * P, (i + 1) * P)
+
+        def score_e(i):
+            ms = rows_of(i)
+            e_sb[i] = ring.tile([P, S], F32, name="e_sb")
+            for hf in range(HALVES):
+                e_bank = bank("e%d_%d" % (i, hf), 2 * (i % 2) + hf)
+                nc.tensor.matmul_mx(
+                    out=e_bank[:], lhsT=v2_w[:, ms].bitcast(FP8X4), lhsT_scale=v2_s[:, ms],
+                    rhs=h_w[hf][:].bitcast(FP8X4), rhs_scale=h_s[hf][:], start=True, stop=True,
+                )
+                nc.vector.tensor_scalar(
+                    out=e_sb[i][:, hf * BANK : (hf + 1) * BANK], in0=e_bank[:], scalar1=1.0, scalar2=None,
+                    op0=ALU.mult, op1=ALU.max, accum_out=tops[:, HALVES * i + hf : HALVES * i + hf + 1],
+                )
+            nc.vector.tensor_scalar(
+                out=bias[:, i : i + 1], in0=tops[:, 2 * i : 2 * i + 1], scalar1=tops[:, 2 * i + 1 : 2 * i + 2],
+                scalar2=shift[:, i : i + 1], op0=ALU.max, op1=ALU.mult,
+            )
+
+        def score_d(i):
+            ms = rows_of(i)
+            if (i * P) % W3_PIECE == 0:
+                quantise_w3(i * P // W3_PIECE)
+            d_sb[i] = ring.tile([P, S], F32, name="d_sb")
+            for hf in range(HALVES):
+                d_bank = bank("d%d_%d" % (i, hf), 4 + 2 * (i % 2) + hf)
+                nc.tensor.matmul_mx(
+                    out=d_bank[:], lhsT=w3_w[:, ms].bitcast(FP8X4), lhsT_scale=w3_s[:, ms],
+                    rhs=h_w[hf][:].bitcast(FP8X4), rhs_scale=h_s[hf][:], start=True, stop=True,
+                )
+                nc.scalar.copy(out=d_sb[i][:, hf * BANK : (hf + 1) * BANK], in_=d_bank[:])
+
+        def look(i):
+            gate[i] = ring.tile([P, NP], F32, name="gate")
+            nc.scalar.activation(
+                out=gate[i][:], in_=e_sb[i][:].indirect(p1[:]), func=ACT.Sigmoid,
+                bias=bias[:, i : i + 1], scale=cols[:, i : i + 1],
+            )
+
+        def pick(i):
+            picked[i] = ring.tile([P, NP], F32, name="picked")
+            nc.vector.tensor_copy(out=picked[i][:], in_=d_sb[i][:].indirect(p2[:]))
+            size[i] = ring.tile([P, NP], F32, name="size")
+            nc.scalar.activation(out=size[i][:], in_=picked[i][:], func=ACT.Abs)
+            gated[i] = ring.tile([P, NP], F32, name="gated")
+            engine = nc.gpsimd if i < ROW_TILES - 1 else nc.vector
+            engine.tensor_tensor(out=gated[i][:], in0=picked[i][:], in1=gate[i][:], op=ALU.mult)
+
+        def finish(i):
+            result = ring.tile([P, NP], F32, name="result")
+            nc.vector.scalar_tensor_tensor(
+                out=result[:], in0=size[i][:], scalar=cols[:, 2 * ROW_TILES + i : 2 * ROW_TILES + i + 1],
+                in1=gated[i][:], op0=ALU.mult, op1=ALU.add,
+            )
+            nc.sync.dma_start(out=out[rows_of(i), :], in_=result[:])
+
+        for step in range(-2, ROW_TILES):
+            if step >= 0:
+                pick(step)
+            if step + 2 < ROW_TILES:
+                score_e(step + 2)
+            if 0 <= step + 1 < ROW_TILES:
+                score_d(step + 1)
+                look(step + 1)
+            if step >= 0:
+                finish(step)

@@ -43,7 +43,7 @@ def tile_list_salt_screen_scores_kernel(
             return keep.tile(shape, dtype, name=name, align_bytes=64)
 
         def tenant(name, shape, dtype, kib):
-            return turns.tile(shape, dtype, name=name, align_bytes=64, offset=kib * 1024)
+            return turns.tile(shape, dtype, name=name, align_bytes=64, offset=int(kib * 1024))
 
         def bank(name, number):
             return psum.tile([P, BANK], F32, name=name, offset=number * BANK * 4)
@@ -53,19 +53,36 @@ def tile_list_salt_screen_scores_kernel(
         p1 = held("p1", [P, NP // 16], U16)
         p2 = held("p2", [P, NP // 16], U16)
 
-        tab_s = tenant("tab_s", [P, T], U8, 52)
+        tab_s = held("tab_s", [P, T], U8)
         tab2_s = held("tab2_s", [P, T3], U8)
         w2_s_raw = held("w2_s_raw", [P, PASSES * H], U8)
-        v_s1 = held("v_s1", [P, S], U8)
-        nc.vector.memset(tab_s[:].bitcast(I32), 0)
-        for plane in (w2_s_raw, tab2_s, v_s1):
-            nc.vector.memset(plane[:].bitcast(I32), 0)
+        v_planes = held("v_planes", [P, PASSES * S], U8)
+        gain_t = held("gain_t", [P, PACK], F32)
+        nc.gpsimd.memset(w2_s_raw[:].bitcast(I32), 0)
+        nc.gpsimd.memset(tab2_s[:].bitcast(I32), 0)
+        for q in range(QUADS):
+            nc.gpsimd.dma_start(
+                out=w2_s_raw[:].bitcast(I32)[32 * q : 32 * q + 4, :].rearrange("p (a c) -> p a c", a=PASSES),
+                in_=w2_scales.bitcast(I32)[:, 4 * q : 4 * q + 4, :].rearrange("a r c -> r a c"),
+            )
+        for q in range(QUADS):
+            nc.gpsimd.dma_start(
+                out=tab2_s[:].bitcast(I32)[32 * q : 32 * q + 4, :],
+                in_=tab2_scales.bitcast(I32)[0, 4 * q : 4 * q + 4, :],
+            )
+        rows = held("rows", [P, P], F32)
+        nc.gpsimd.memset(rows[:], 0.0)
+        for n, vec in enumerate((steep, share, lat)):
+            nc.gpsimd.dma_start(out=rows[ROW_TILES * n : ROW_TILES * (n + 1), :], in_=vec.rearrange("(i p) -> i p", p=P))
+        for q in range(QUADS):
+            nc.vector.memset(tab_s[:].bitcast(I32)[32 * q : 32 * q + 24, :], 0)
+        nc.vector.memset(v_planes[:].bitcast(I32)[96:128, :], 0)
         ident = held("ident", [P, P], F32)
         make_identity(nc, ident[:])
 
-        tab_w = [tenant("tab_w0", [P, T], I32, 0)]
-        w1_raw = [tenant("w1_raw%d" % a, [P, PACK, H], F32, 16 + 8 * a) for a in range(PASSES)]
-        w2_raw = held("w2_raw", [P, PASSES, H], U16)
+        tab_w = [tenant("tab_w0", [P, T], I32, 8)]
+        w1_raw = [tenant("w1_raw%d" % a, [P, PACK, H], F32, 24 + 8 * a) for a in range(PASSES)]
+        w2_raw = tenant("w2_raw", [P, PASSES, H], U16, 67)
         w3_cols = S2 // W3_LOADS
 
         def load_words(tile, words):
@@ -74,43 +91,35 @@ def tile_list_salt_screen_scores_kernel(
         def load_w1(a):
             nc.sync.dma_start(out=w1_raw[a][:], in_=w1[a * 512 : (a + 1) * 512, :].rearrange("(p j) c -> p j c", j=PACK))
 
-        for tile, source in ((idx, offs), (idx2, offs2), (p1, pos1), (p2, pos2)):
+        for tile, source in ((idx, offs), (idx2, offs2), (p1, pos1)):
             nc.sync.dma_start(out=tile[:], in_=source)
+        for q in range(QUADS):
+            nc.sync.dma_start(
+                out=tab_s[:].bitcast(I32)[32 * q + 24 : 32 * q + 32, :],
+                in_=tab_scales.bitcast(I32)[:, 4 * q : 4 * q + 4, :],
+            )
         load_words(tab_w[0], tab_words[0])
         nc.sync.dma_start(
             out=w2_raw[:].rearrange("p a c -> p (a c)").bitcast(I32).rearrange("p (a c) -> p a c", a=PASSES),
             in_=w2_words.bitcast(I32).rearrange("a p c -> p a c"),
         )
         load_w1(0)
+        nc.sync.dma_start(out=p2[:], in_=pos2)
+        nc.sync.dma_start(out=gain_t[:], in_=gain.rearrange("(p t) -> p t", t=PACK))
         load_w1(1)
-        for q in range(QUADS):
-            nc.scalar.dma_start(
-                out=tab_s[:].bitcast(I32)[32 * q : 32 * q + 8, :],
-                in_=tab_scales.bitcast(I32)[:, 4 * q : 4 * q + 4, :],
-            )
-        for q in range(QUADS):
-            nc.gpsimd.dma_start(
-                out=w2_s_raw[:].bitcast(I32)[32 * q : 32 * q + 4, :].rearrange("p (a c) -> p a c", a=PASSES),
-                in_=w2_scales.bitcast(I32)[:, 4 * q : 4 * q + 4, :].rearrange("a r c -> r a c"),
-            )
 
         v_s = held("v_s", [P, S], U8)
         nc.vector.tensor_copy(out=v_s[:], in_=tab_s[:].indirect(idx[:]))
-        nc.gpsimd.dma_start(out=v_s1[:].bitcast(I32)[0:100, :], in_=v_s[:].bitcast(I32)[4:104, :])
-        rows = tenant("rows", [P, P], F32, 52)
-        gain_t = tenant("gain_t", [P, PACK], F32, 53)
-        nc.vector.memset(rows[:], 0.0)
-        v_scale = [v_s, v_s1]
-        for q in range(QUADS):
-            nc.gpsimd.dma_start(
-                out=tab2_s[:].bitcast(I32)[32 * q : 32 * q + 4, :],
-                in_=tab2_scales.bitcast(I32)[0, 4 * q : 4 * q + 4, :],
+        for a in range(PASSES):
+            nc.sync.dma_start(
+                out=v_planes[:, a * S : (a + 1) * S].bitcast(I32)[0:100, :],
+                in_=v_s[:].bitcast(I32)[24 + 4 * a : 124 + 4 * a, :],
             )
-        nc.gpsimd.dma_start(out=gain_t[:], in_=gain.rearrange("(p t) -> p t", t=PACK))
-        for n, vec in enumerate((steep, share, lat)):
-            nc.gpsimd.dma_start(out=rows[ROW_TILES * n : ROW_TILES * (n + 1), :], in_=vec.rearrange("(i p) -> i p", p=P))
 
-        v_w = [[held("v_w%d_%d" % (a, hf), [P, BANK], U32) for hf in range(HALVES)] for a in range(PASSES)]
+        v_w = [
+            [held("v_w0_%d" % hf, [P, BANK], U32) for hf in range(HALVES)],
+            [tenant("v_w1_%d" % hf, [P, BANK], U32, 49 + 2 * hf) for hf in range(HALVES)],
+        ]
 
         def gather_v(a, hf):
             nc.vector.tensor_copy(
@@ -120,42 +129,43 @@ def tile_list_salt_screen_scores_kernel(
 
         for hf in range(HALVES):
             gather_v(0, hf)
+        w2_s = tenant("w2_s", [P, PASSES * H], U8, 18)
+        nc.vector.tensor_copy(
+            out=w2_s[:].rearrange("p (a t m) -> p a t m", a=PASSES, t=PACK),
+            in_=w2_s_raw[:].rearrange("p (a m t) -> p a t m", a=PASSES, t=PACK),
+        )
         tab_w.append(tenant("tab_w1", [P, T], I32, 0))
         load_words(tab_w[1], tab_words[1])
 
-        w2_w = held("w2_w", [P, PASSES, H], U16)
-        w2_s = held("w2_s", [P, PASSES * H], U8)
+        w2_w = tenant("w2_w", [P, PASSES, H], U16, 16)
         for a in range(PASSES):
             nc.vector.tensor_copy(
                 out=w2_w[:, a, :].rearrange("p (t m) -> p t m", t=PACK),
                 in_=w2_raw[:, a, :].rearrange("p (m t) -> p t m", t=PACK),
             )
-        nc.vector.tensor_copy(
-            out=w2_s[:].rearrange("p (a t m) -> p a t m", a=PASSES, t=PACK),
-            in_=w2_s_raw[:].rearrange("p (a m t) -> p a t m", a=PASSES, t=PACK),
-        )
 
-        v2_s = held("v2_s", [P, S2], U8)
+        v2_s = tenant("v2_s", [P, S2], U8, 19)
         nc.vector.tensor_copy(out=v2_s[:], in_=tab2_s[:].indirect(idx2[:]))
 
-        w1_w = [held("w1_w%d" % a, [P, H], U32) for a in range(PASSES)]
+        w1_w = [tenant("w1_w%d" % a, [P, H], U32, 20 + 2 * a) for a in range(PASSES)]
         w1_s = [held("w1_s%d" % a, [P, H], U8) for a in range(PASSES)]
         for a in range(PASSES):
-            w1_bf = tenant("w1_bf%d" % a, [P, H * PACK], BF16, 32 + 8 * a)
+            w1_bf = tenant("w1_bf%d" % a, [P, H * PACK], BF16, 40 + 9 * a)
             nc.scalar.copy(
                 out=w1_bf[:].rearrange("p (t m j) -> p m t j", t=PACK, j=PACK),
                 in_=w1_raw[a][:].rearrange("p j (m t) -> p m t j", t=PACK),
             )
             nc.vector.quantize_mx(out=w1_w[a][:].bitcast(FP8X4), scales=w1_s[a][:], in_=w1_bf[:])
-        tab2_w = tenant("tab2_w", [P, T3], I32, 16)
+        tab2_w = tenant("tab2_w", [P, T3], I32, 67)
         load_words(tab2_w, tab2_words[0])
         w3_raw = []
         for b in range(W3_LOADS):
-            w3_raw.append(tenant("w3_raw%d" % b, [P, PACK, w3_cols], F32, 32 - 8 * b))
+            w3_raw.append(tenant("w3_raw%d" % b, [P, PACK, w3_cols], F32, 41 - 8.5 * b))
             nc.sync.dma_start(
                 out=w3_raw[b][:],
                 in_=w3[:, b * w3_cols : (b + 1) * w3_cols].rearrange("(p j) c -> p j c", j=PACK),
             )
+
 
         for hf in range(HALVES):
             gather_v(1, hf)
@@ -165,46 +175,70 @@ def tile_list_salt_screen_scores_kernel(
         h_s = [held("h_s%d" % hf, [P, BANK], U8) for hf in range(HALVES)]
         v2_w = tenant("v2_w", [P, S2], U32, 0)
 
-        for hf in range(HALVES):
-            cs = slice(hf * BANK, (hf + 1) * BANK)
-            f_bank = [bank("f%d_%d" % (hf, t), t) for t in range(PACK)]
-            g_bank = [bank("g%d_%d" % (hf, t), PACK + t) for t in range(PACK)]
-            steps = [(a, t) for a in range(PASSES) for t in range(PACK)]
-            if hf > 0:
-                steps = sorted(steps, key=lambda step: (step[1], step[0]))
-            for a, t in steps:
-                if True:
-                    nc.tensor.matmul_mx(
-                        out=f_bank[t][:], lhsT=w1_w[a][:, t * P : (t + 1) * P].bitcast(FP8X4),
-                        lhsT_scale=w1_s[a][:, t * P : (t + 1) * P],
-                        rhs=v_w[a][hf][:].bitcast(FP8X4), rhs_scale=v_scale[a][:, cs],
-                        start=(a == 0), stop=(a == PASSES - 1),
-                    )
-                    nc.tensor.matmul_mx(
-                        out=g_bank[t][:], lhsT=w2_w[:, a, t * P : (t + 1) * P].bitcast(FP4X4),
-                        lhsT_scale=w2_s[:, a * H + t * P : a * H + (t + 1) * P],
-                        rhs=v_w[a][hf][:].bitcast(FP8X4), rhs_scale=v_scale[a][:, cs],
-                        start=(a == 0), stop=(a == PASSES - 1),
-                    )
-            h_planes = held("h_planes%d" % hf, [P, PACK, BANK], BF16)
-            for t in range(PACK):
-                bent = ring.tile([P, BANK], F32, name="bent")
-                nc.scalar.activation(out=bent[:], in_=f_bank[t][:], func=ACT.Silu)
-                nc.vector.scalar_tensor_tensor(
-                    out=h_planes[:, t, :], in0=bent[:], scalar=gain_t[:, t : t + 1], in1=g_bank[t][:],
-                    op0=ALU.mult, op1=ALU.add,
-                )
-            h_bf = tenant("h_bf%d" % hf, [P, BANK * PACK], BF16, 44 + 4 * hf)
-            nc.scalar.copy(
-                out=h_bf[:].rearrange("p (c i t) -> p c t i", i=4, t=PACK),
-                in_=h_planes[:].rearrange("p t (c i) -> p c t i", i=4),
-            )
-            nc.vector.quantize_mx(out=h_w[hf][:].bitcast(FP8X4), scales=h_s[hf][:], in_=h_bf[:])
-            nc.vector.tensor_copy(
-                out=v2_w[:, cs], in_=tab2_w[:].bitcast(U32).indirect(idx2[:, hf * 32 : (hf + 1) * 32]),
+        def v_scales(a, hf):
+            return v_planes[:, a * S + hf * BANK : a * S + (hf + 1) * BANK]
+
+        f_bank = {(hf, t): bank("f%d_%d" % (hf, t), PACK * hf + t) for hf in range(HALVES) for t in range(PACK)}
+        bent = {}
+        h_planes = [held("h_planes%d" % hf, [P, PACK, BANK], BF16) for hf in range(HALVES)]
+
+        def f_pass(a, hf, t):
+            nc.tensor.matmul_mx(
+                out=f_bank[hf, t][:], lhsT=w1_w[a][:, t * P : (t + 1) * P].bitcast(FP8X4),
+                lhsT_scale=w1_s[a][:, t * P : (t + 1) * P],
+                rhs=v_w[a][hf][:].bitcast(FP8X4), rhs_scale=v_scales(a, hf),
+                start=(a == 0), stop=(a == PASSES - 1),
             )
 
-        turned = bank("turned", 2)
+        def bend(hf, t):
+            f_pass(1, hf, t)
+            bent[hf, t] = tenant("bent%d_%d" % (hf, t), [P, BANK], F32, 76 + 2 * (PACK * hf + t))
+            nc.scalar.activation(out=bent[hf, t][:], in_=f_bank[hf, t][:], func=ACT.Silu)
+
+        def feature(hf, t):
+            g_bank = bank("g%d_%d" % (hf, t), PACK * hf + t)
+            for a in range(PASSES):
+                nc.tensor.matmul_mx(
+                    out=g_bank[:], lhsT=w2_w[:, a, t * P : (t + 1) * P].bitcast(FP4X4),
+                    lhsT_scale=w2_s[:, a * H + t * P : a * H + (t + 1) * P],
+                    rhs=v_w[a][hf][:].bitcast(FP8X4), rhs_scale=v_scales(a, hf),
+                    start=(a == 0), stop=(a == PASSES - 1),
+                )
+            nc.vector.scalar_tensor_tensor(
+                out=h_planes[hf][:, t, :], in0=bent[hf, t][:], scalar=gain_t[:, t : t + 1], in1=g_bank[:],
+                op0=ALU.mult, op1=ALU.add,
+            )
+
+        def quantise_h(hf, weave):
+            h_bf = tenant("h_bf%d" % hf, [P, BANK * PACK], BF16, 53 + 4 * hf)
+            weave(
+                out=h_bf[:].rearrange("p (c i t) -> p c t i", i=4, t=PACK),
+                in_=h_planes[hf][:].rearrange("p t (c i) -> p c t i", i=4),
+            )
+            nc.vector.quantize_mx(out=h_w[hf][:].bitcast(FP8X4), scales=h_s[hf][:], in_=h_bf[:])
+
+        def gather_v2(hf):
+            nc.vector.tensor_copy(
+                out=v2_w[:, hf * BANK : (hf + 1) * BANK],
+                in_=tab2_w[:].bitcast(U32).indirect(idx2[:, hf * 32 : (hf + 1) * 32]),
+            )
+
+        for hf in range(HALVES):
+            for t in range(PACK):
+                f_pass(0, hf, t)
+        for t in range(PACK):
+            bend(0, t)
+        for t in range(PACK):
+            bend(1, t)
+            feature(0, t)
+        for t in range(PACK):
+            feature(1, t)
+        quantise_h(0, nc.scalar.copy)
+        quantise_h(1, nc.vector.tensor_copy)
+        for hf in range(HALVES):
+            gather_v2(hf)
+
+        turned = bank("turned", 7)
         nc.tensor.transpose(turned[:, :P], rows[:], ident[:])
         cols = held("cols", [P, 3 * ROW_TILES], F32)
         nc.scalar.copy(out=cols[:], in_=turned[:, : 3 * ROW_TILES])
@@ -214,19 +248,17 @@ def tile_list_salt_screen_scores_kernel(
             out=shift[:], in0=cols[:, :ROW_TILES], scalar=-1.0, in1=cols[:, ROW_TILES : 2 * ROW_TILES],
             op0=ALU.mult, op1=ALU.mult,
         )
-        w3_w = tenant("w3_w", [P, S2], U32, 48)
+        w3_w = tenant("w3_w", [P, S2], U32, 57)
         w3_s = held("w3_s", [P, S2], U8)
 
         def quantise_w3(piece):
             c0 = piece * W3_PIECE
             b, off = divmod(c0, w3_cols)
-            w3_bf = held("w3_bf%d" % piece, [P, W3_PIECE * PACK], BF16)
-            for part in range(W3_PIECE // P):
-                nc.gpsimd.tensor_scalar(
-                    out=w3_bf[:, part * P * PACK : (part + 1) * P * PACK].rearrange("p (c j) -> p c j", j=PACK),
-                    in0=w3_raw[b][:, :, off + part * P : off + (part + 1) * P].rearrange("p j c -> p c j"),
-                    scalar1=1.0, scalar2=0.0, op0=ALU.mult, op1=ALU.add,
-                )
+            w3_bf = tenant("w3_bf%d" % piece, [P, W3_PIECE * PACK], BF16, 82 + 2 * (piece % 2))
+            nc.scalar.copy(
+                out=w3_bf[:].rearrange("p (c i j) -> p c j i", i=4, j=PACK),
+                in_=w3_raw[b][:, :, off : off + W3_PIECE].rearrange("p j (c i) -> p c j i", i=4),
+            )
             nc.vector.quantize_mx(
                 out=w3_w[:, c0 : c0 + W3_PIECE].bitcast(FP8X4), scales=w3_s[:, c0 : c0 + W3_PIECE], in_=w3_bf[:],
             )
@@ -251,7 +283,7 @@ def tile_list_salt_screen_scores_kernel(
                     out=e_sb[i][:, hf * BANK : (hf + 1) * BANK], in0=e_bank[:], scalar1=1.0, scalar2=None,
                     op0=ALU.mult, op1=ALU.max, accum_out=tops[:, HALVES * i + hf : HALVES * i + hf + 1],
                 )
-            nc.vector.tensor_scalar(
+            nc.gpsimd.tensor_scalar(
                 out=bias[:, i : i + 1], in0=tops[:, 2 * i : 2 * i + 1], scalar1=tops[:, 2 * i + 1 : 2 * i + 2],
                 scalar2=shift[:, i : i + 1], op0=ALU.max, op1=ALU.mult,
             )
@@ -282,8 +314,7 @@ def tile_list_salt_screen_scores_kernel(
             size[i] = ring.tile([P, NP], F32, name="size")
             nc.scalar.activation(out=size[i][:], in_=picked[i][:], func=ACT.Abs)
             gated[i] = ring.tile([P, NP], F32, name="gated")
-            engine = nc.gpsimd if i < ROW_TILES - 1 else nc.vector
-            engine.tensor_tensor(out=gated[i][:], in0=picked[i][:], in1=gate[i][:], op=ALU.mult)
+            nc.vector.tensor_tensor(out=gated[i][:], in0=picked[i][:], in1=gate[i][:], op=ALU.mult)
 
         def finish(i):
             result = ring.tile([P, NP], F32, name="result")

@@ -58,22 +58,13 @@ def tile_list_salt_screen_scores_kernel(
         w2_s_raw = held("w2_s_raw", [P, PASSES * H], U8)
         v_planes = held("v_planes", [P, PASSES * S], U8)
         gain_t = held("gain_t", [P, PACK], F32)
-        nc.gpsimd.memset(w2_s_raw[:].bitcast(I32), 0)
+        nc.vector.memset(w2_s_raw[:].bitcast(I32), 0)
         nc.gpsimd.memset(tab2_s[:].bitcast(I32), 0)
-        for q in range(QUADS):
-            nc.gpsimd.dma_start(
-                out=w2_s_raw[:].bitcast(I32)[32 * q : 32 * q + 4, :].rearrange("p (a c) -> p a c", a=PASSES),
-                in_=w2_scales.bitcast(I32)[:, 4 * q : 4 * q + 4, :].rearrange("a r c -> r a c"),
-            )
         for q in range(QUADS):
             nc.gpsimd.dma_start(
                 out=tab2_s[:].bitcast(I32)[32 * q : 32 * q + 4, :],
                 in_=tab2_scales.bitcast(I32)[0, 4 * q : 4 * q + 4, :],
             )
-        rows = held("rows", [P, P], F32)
-        nc.gpsimd.memset(rows[:], 0.0)
-        for n, vec in enumerate((steep, share, lat)):
-            nc.gpsimd.dma_start(out=rows[ROW_TILES * n : ROW_TILES * (n + 1), :], in_=vec.rearrange("(i p) -> i p", p=P))
         for q in range(QUADS):
             nc.vector.memset(tab_s[:].bitcast(I32)[32 * q : 32 * q + 24, :], 0)
         nc.vector.memset(v_planes[:].bitcast(I32)[96:128, :], 0)
@@ -107,6 +98,11 @@ def tile_list_salt_screen_scores_kernel(
         nc.sync.dma_start(out=p2[:], in_=pos2)
         nc.sync.dma_start(out=gain_t[:], in_=gain.rearrange("(p t) -> p t", t=PACK))
         load_w1(1)
+        for q in range(QUADS):
+            nc.scalar.dma_start(
+                out=w2_s_raw[:].bitcast(I32)[32 * q : 32 * q + 4, :].rearrange("p (a c) -> p a c", a=PASSES),
+                in_=w2_scales.bitcast(I32)[:, 4 * q : 4 * q + 4, :].rearrange("a r c -> r a c"),
+            )
 
         v_s = held("v_s", [P, S], U8)
         nc.vector.tensor_copy(out=v_s[:], in_=tab_s[:].indirect(idx[:]))
@@ -118,7 +114,7 @@ def tile_list_salt_screen_scores_kernel(
 
         v_w = [
             [held("v_w0_%d" % hf, [P, BANK], U32) for hf in range(HALVES)],
-            [tenant("v_w1_%d" % hf, [P, BANK], U32, 49 + 2 * hf) for hf in range(HALVES)],
+            [tenant("v_w1_%d" % hf, [P, BANK], U32, 51.5 + 2 * hf) for hf in range(HALVES)],
         ]
 
         def gather_v(a, hf):
@@ -129,11 +125,6 @@ def tile_list_salt_screen_scores_kernel(
 
         for hf in range(HALVES):
             gather_v(0, hf)
-        w2_s = tenant("w2_s", [P, PASSES * H], U8, 18)
-        nc.vector.tensor_copy(
-            out=w2_s[:].rearrange("p (a t m) -> p a t m", a=PASSES, t=PACK),
-            in_=w2_s_raw[:].rearrange("p (a m t) -> p a t m", a=PASSES, t=PACK),
-        )
         tab_w.append(tenant("tab_w1", [P, T], I32, 0))
         load_words(tab_w[1], tab_words[1])
 
@@ -144,13 +135,11 @@ def tile_list_salt_screen_scores_kernel(
                 in_=w2_raw[:, a, :].rearrange("p (m t) -> p t m", t=PACK),
             )
 
-        v2_s = tenant("v2_s", [P, S2], U8, 19)
-        nc.vector.tensor_copy(out=v2_s[:], in_=tab2_s[:].indirect(idx2[:]))
 
         w1_w = [tenant("w1_w%d" % a, [P, H], U32, 20 + 2 * a) for a in range(PASSES)]
         w1_s = [held("w1_s%d" % a, [P, H], U8) for a in range(PASSES)]
         for a in range(PASSES):
-            w1_bf = tenant("w1_bf%d" % a, [P, H * PACK], BF16, 40 + 9 * a)
+            w1_bf = tenant("w1_bf%d" % a, [P, H * PACK], BF16, 40 + 11 * a)
             nc.scalar.copy(
                 out=w1_bf[:].rearrange("p (t m j) -> p m t j", t=PACK, j=PACK),
                 in_=w1_raw[a][:].rearrange("p j (m t) -> p m t j", t=PACK),
@@ -160,13 +149,24 @@ def tile_list_salt_screen_scores_kernel(
         load_words(tab2_w, tab2_words[0])
         w3_raw = []
         for b in range(W3_LOADS):
-            w3_raw.append(tenant("w3_raw%d" % b, [P, PACK, w3_cols], F32, 41 - 8.5 * b))
+            w3_raw.append(tenant("w3_raw%d" % b, [P, PACK, w3_cols], F32, 42 - 9.5 * b))
             nc.sync.dma_start(
                 out=w3_raw[b][:],
                 in_=w3[:, b * w3_cols : (b + 1) * w3_cols].rearrange("(p j) c -> p j c", j=PACK),
             )
 
 
+        w2_s = tenant("w2_s", [P, PASSES * H], U8, 40.5)
+        nc.vector.tensor_copy(
+            out=w2_s[:].rearrange("p (a t m) -> p a t m", a=PASSES, t=PACK),
+            in_=w2_s_raw[:].rearrange("p (a m t) -> p a t m", a=PASSES, t=PACK),
+        )
+        rows = tenant("rows", [P, P], F32, 41.5)
+        nc.vector.memset(rows[:], 0.0)
+        for n, vec in enumerate((steep, share, lat)):
+            nc.sync.dma_start(out=rows[ROW_TILES * n : ROW_TILES * (n + 1), :], in_=vec.rearrange("(i p) -> i p", p=P))
+        v2_s = tenant("v2_s", [P, S2], U8, 50.5)
+        nc.vector.tensor_copy(out=v2_s[:], in_=tab2_s[:].indirect(idx2[:]))
         for hf in range(HALVES):
             gather_v(1, hf)
 
@@ -210,7 +210,7 @@ def tile_list_salt_screen_scores_kernel(
             )
 
         def quantise_h(hf, weave):
-            h_bf = tenant("h_bf%d" % hf, [P, BANK * PACK], BF16, 53 + 4 * hf)
+            h_bf = tenant("h_bf%d" % hf, [P, BANK * PACK], BF16, 56 + 4 * hf)
             weave(
                 out=h_bf[:].rearrange("p (c i t) -> p c t i", i=4, t=PACK),
                 in_=h_planes[hf][:].rearrange("p t (c i) -> p c t i", i=4),
@@ -248,7 +248,7 @@ def tile_list_salt_screen_scores_kernel(
             out=shift[:], in0=cols[:, :ROW_TILES], scalar=-1.0, in1=cols[:, ROW_TILES : 2 * ROW_TILES],
             op0=ALU.mult, op1=ALU.mult,
         )
-        w3_w = tenant("w3_w", [P, S2], U32, 57)
+        w3_w = tenant("w3_w", [P, S2], U32, 60)
         w3_s = held("w3_s", [P, S2], U8)
 
         def quantise_w3(piece):
@@ -280,12 +280,13 @@ def tile_list_salt_screen_scores_kernel(
                     rhs=h_w[hf][:].bitcast(FP8X4), rhs_scale=h_s[hf][:], start=True, stop=True,
                 )
                 nc.vector.tensor_scalar(
-                    out=e_sb[i][:, hf * BANK : (hf + 1) * BANK], in0=e_bank[:], scalar1=1.0, scalar2=None,
+                    out=e_sb[i][:, hf * BANK : (hf + 1) * BANK], in0=e_bank[:], scalar1=1.0,
+                    scalar2=None if hf == 0 else tops[:, HALVES * i : HALVES * i + 1],
                     op0=ALU.mult, op1=ALU.max, accum_out=tops[:, HALVES * i + hf : HALVES * i + hf + 1],
                 )
-            nc.gpsimd.tensor_scalar(
-                out=bias[:, i : i + 1], in0=tops[:, 2 * i : 2 * i + 1], scalar1=tops[:, 2 * i + 1 : 2 * i + 2],
-                scalar2=shift[:, i : i + 1], op0=ALU.max, op1=ALU.mult,
+            nc.scalar.activation(
+                out=bias[:, i : i + 1], in_=tops[:, HALVES * i + 1 : HALVES * i + 2], func=ACT.Copy,
+                scale=shift[:, i : i + 1],
             )
 
         def score_d(i):

@@ -59,14 +59,15 @@ def tile_list_salt_screen_scores_kernel(
         v_planes = held("v_planes", [P, PASSES * S], U8)
         gain_t = held("gain_t", [P, PACK], F32)
         nc.vector.memset(w2_s_raw[:].bitcast(I32), 0)
+        for q in range(QUADS):
+            engine = nc.vector if q < QUADS // 2 else nc.gpsimd
+            engine.memset(tab_s[:].bitcast(I32)[32 * q : 32 * q + 24, :], 0)
         nc.gpsimd.memset(tab2_s[:].bitcast(I32), 0)
         for q in range(QUADS):
             nc.gpsimd.dma_start(
                 out=tab2_s[:].bitcast(I32)[32 * q : 32 * q + 4, :],
                 in_=tab2_scales.bitcast(I32)[0, 4 * q : 4 * q + 4, :],
             )
-        for q in range(QUADS):
-            nc.vector.memset(tab_s[:].bitcast(I32)[32 * q : 32 * q + 24, :], 0)
         nc.vector.memset(v_planes[:].bitcast(I32)[96:128, :], 0)
         ident = held("ident", [P, P], F32)
         make_identity(nc, ident[:])
@@ -114,7 +115,7 @@ def tile_list_salt_screen_scores_kernel(
 
         v_w = [
             [held("v_w0_%d" % hf, [P, BANK], U32) for hf in range(HALVES)],
-            [tenant("v_w1_%d" % hf, [P, BANK], U32, 51.5 + 2 * hf) for hf in range(HALVES)],
+            [tenant("v_w1_%d" % hf, [P, BANK], U32, 51 + 2 * hf) for hf in range(HALVES)],
         ]
 
         def gather_v(a, hf):
@@ -149,7 +150,7 @@ def tile_list_salt_screen_scores_kernel(
         load_words(tab2_w, tab2_words[0])
         w3_raw = []
         for b in range(W3_LOADS):
-            w3_raw.append(tenant("w3_raw%d" % b, [P, PACK, w3_cols], F32, 42 - 9.5 * b))
+            w3_raw.append(tenant("w3_raw%d" % b, [P, PACK, w3_cols], F32, 43 - 10.5 * b))
             nc.sync.dma_start(
                 out=w3_raw[b][:],
                 in_=w3[:, b * w3_cols : (b + 1) * w3_cols].rearrange("(p j) c -> p j c", j=PACK),
@@ -165,7 +166,7 @@ def tile_list_salt_screen_scores_kernel(
         nc.vector.memset(rows[:], 0.0)
         for n, vec in enumerate((steep, share, lat)):
             nc.sync.dma_start(out=rows[ROW_TILES * n : ROW_TILES * (n + 1), :], in_=vec.rearrange("(i p) -> i p", p=P))
-        v2_s = tenant("v2_s", [P, S2], U8, 50.5)
+        v2_s = tenant("v2_s", [P, S2], U8, 42)
         nc.vector.tensor_copy(out=v2_s[:], in_=tab2_s[:].indirect(idx2[:]))
         for hf in range(HALVES):
             gather_v(1, hf)
@@ -254,7 +255,7 @@ def tile_list_salt_screen_scores_kernel(
         def quantise_w3(piece):
             c0 = piece * W3_PIECE
             b, off = divmod(c0, w3_cols)
-            w3_bf = tenant("w3_bf%d" % piece, [P, W3_PIECE * PACK], BF16, 82 + 2 * (piece % 2))
+            w3_bf = tenant("w3_bf%d" % piece, [P, W3_PIECE * PACK], BF16, 82 + 2 * piece)
             nc.scalar.copy(
                 out=w3_bf[:].rearrange("p (c i j) -> p c j i", i=4, j=PACK),
                 in_=w3_raw[b][:, :, off : off + W3_PIECE].rearrange("p j (c i) -> p c j i", i=4),
@@ -270,23 +271,19 @@ def tile_list_salt_screen_scores_kernel(
         def rows_of(i):
             return slice(i * P, (i + 1) * P)
 
-        def score_e(i):
+        def score_e(i, hf):
             ms = rows_of(i)
-            e_sb[i] = ring.tile([P, S], F32, name="e_sb")
-            for hf in range(HALVES):
-                e_bank = bank("e%d_%d" % (i, hf), 2 * (i % 2) + hf)
-                nc.tensor.matmul_mx(
-                    out=e_bank[:], lhsT=v2_w[:, ms].bitcast(FP8X4), lhsT_scale=v2_s[:, ms],
-                    rhs=h_w[hf][:].bitcast(FP8X4), rhs_scale=h_s[hf][:], start=True, stop=True,
-                )
-                nc.vector.tensor_scalar(
-                    out=e_sb[i][:, hf * BANK : (hf + 1) * BANK], in0=e_bank[:], scalar1=1.0,
-                    scalar2=None if hf == 0 else tops[:, HALVES * i : HALVES * i + 1],
-                    op0=ALU.mult, op1=ALU.max, accum_out=tops[:, HALVES * i + hf : HALVES * i + hf + 1],
-                )
-            nc.scalar.activation(
-                out=bias[:, i : i + 1], in_=tops[:, HALVES * i + 1 : HALVES * i + 2], func=ACT.Copy,
-                scale=shift[:, i : i + 1],
+            if hf == 0:
+                e_sb[i] = ring.tile([P, S], F32, name="e_sb", bufs=2)
+            e_bank = bank("e%d_%d" % (i, hf), 2 * (i % 2) + hf)
+            nc.tensor.matmul_mx(
+                out=e_bank[:], lhsT=v2_w[:, ms].bitcast(FP8X4), lhsT_scale=v2_s[:, ms],
+                rhs=h_w[hf][:].bitcast(FP8X4), rhs_scale=h_s[hf][:], start=True, stop=True,
+            )
+            nc.vector.tensor_scalar(
+                out=e_sb[i][:, hf * BANK : (hf + 1) * BANK], in0=e_bank[:], scalar1=1.0,
+                scalar2=None if hf == 0 else tops[:, HALVES * i : HALVES * i + 1],
+                op0=ALU.mult, op1=ALU.max, accum_out=tops[:, HALVES * i + hf : HALVES * i + hf + 1],
             )
 
         def score_d(i):
@@ -303,6 +300,10 @@ def tile_list_salt_screen_scores_kernel(
                 nc.scalar.copy(out=d_sb[i][:, hf * BANK : (hf + 1) * BANK], in_=d_bank[:])
 
         def look(i):
+            nc.scalar.activation(
+                out=bias[:, i : i + 1], in_=tops[:, HALVES * i + 1 : HALVES * i + 2], func=ACT.Copy,
+                scale=shift[:, i : i + 1],
+            )
             gate[i] = ring.tile([P, NP], F32, name="gate")
             nc.scalar.activation(
                 out=gate[i][:], in_=e_sb[i][:].indirect(p1[:]), func=ACT.Sigmoid,
@@ -314,6 +315,8 @@ def tile_list_salt_screen_scores_kernel(
             nc.vector.tensor_copy(out=picked[i][:], in_=d_sb[i][:].indirect(p2[:]))
             size[i] = ring.tile([P, NP], F32, name="size")
             nc.scalar.activation(out=size[i][:], in_=picked[i][:], func=ACT.Abs)
+
+        def pass_gate(i):
             gated[i] = ring.tile([P, NP], F32, name="gated")
             nc.vector.tensor_tensor(out=gated[i][:], in0=picked[i][:], in1=gate[i][:], op=ALU.mult)
 
@@ -325,13 +328,18 @@ def tile_list_salt_screen_scores_kernel(
             )
             nc.sync.dma_start(out=out[rows_of(i), :], in_=result[:])
 
-        for step in range(-2, ROW_TILES):
-            if step >= 0:
+        for step in range(-1, ROW_TILES):
+            now, ahead = step >= 0, step + 1 < ROW_TILES
+            if now:
                 pick(step)
-            if step + 2 < ROW_TILES:
-                score_e(step + 2)
-            if 0 <= step + 1 < ROW_TILES:
+            if ahead:
+                score_e(step + 1, 0)
+            if now:
+                pass_gate(step)
+            if ahead:
                 score_d(step + 1)
-                look(step + 1)
-            if step >= 0:
+                score_e(step + 1, 1)
+            if now:
                 finish(step)
+            if ahead:
+                look(step + 1)

@@ -255,11 +255,20 @@ def tile_list_salt_screen_scores_kernel(
         def quantise_w3(piece):
             c0 = piece * W3_PIECE
             b, off = divmod(c0, w3_cols)
-            w3_bf = tenant("w3_bf%d" % piece, [P, W3_PIECE * PACK], BF16, 82 + 2 * piece)
-            nc.scalar.copy(
-                out=w3_bf[:].rearrange("p (c i j) -> p c j i", i=4, j=PACK),
-                in_=w3_raw[b][:, :, off : off + W3_PIECE].rearrange("p j (c i) -> p c j i", i=4),
-            )
+            if b == 0:
+                w3_bf = held("w3_bf%d" % piece, [P, W3_PIECE * PACK], BF16)
+                for c in range(0, W3_PIECE, P):
+                    nc.gpsimd.tensor_scalar(
+                        out=w3_bf[:, c * PACK : (c + P) * PACK].rearrange("p (c j) -> p c j", j=PACK),
+                        in0=w3_raw[b][:, :, off + c : off + c + P].rearrange("p j c -> p c j"),
+                        scalar1=1.0, scalar2=0.0, op0=ALU.mult, op1=ALU.add,
+                    )
+            else:
+                w3_bf = tenant("w3_bf%d" % piece, [P, W3_PIECE * PACK], BF16, 78 + 2 * piece)
+                nc.scalar.copy(
+                    out=w3_bf[:].rearrange("p (c i j) -> p c j i", i=4, j=PACK),
+                    in_=w3_raw[b][:, :, off : off + W3_PIECE].rearrange("p j (c i) -> p c j i", i=4),
+                )
             nc.vector.quantize_mx(
                 out=w3_w[:, c0 : c0 + W3_PIECE].bitcast(FP8X4), scales=w3_s[:, c0 : c0 + W3_PIECE], in_=w3_bf[:],
             )
@@ -274,7 +283,7 @@ def tile_list_salt_screen_scores_kernel(
         def score_e(i, hf):
             ms = rows_of(i)
             if hf == 0:
-                e_sb[i] = ring.tile([P, S], F32, name="e_sb", bufs=2)
+                e_sb[i] = ring.tile([P, S], F32, name="e_sb")
             e_bank = bank("e%d_%d" % (i, hf), 2 * (i % 2) + hf)
             nc.tensor.matmul_mx(
                 out=e_bank[:], lhsT=v2_w[:, ms].bitcast(FP8X4), lhsT_scale=v2_s[:, ms],
@@ -299,47 +308,56 @@ def tile_list_salt_screen_scores_kernel(
                 )
                 nc.scalar.copy(out=d_sb[i][:, hf * BANK : (hf + 1) * BANK], in_=d_bank[:])
 
-        def look(i):
+        def make_bias(i):
             nc.scalar.activation(
                 out=bias[:, i : i + 1], in_=tops[:, HALVES * i + 1 : HALVES * i + 2], func=ACT.Copy,
                 scale=shift[:, i : i + 1],
             )
+
+        def look(i):
             gate[i] = ring.tile([P, NP], F32, name="gate")
             nc.scalar.activation(
                 out=gate[i][:], in_=e_sb[i][:].indirect(p1[:]), func=ACT.Sigmoid,
                 bias=bias[:, i : i + 1], scale=cols[:, i : i + 1],
             )
 
-        def pick(i):
-            picked[i] = ring.tile([P, NP], F32, name="picked")
-            nc.vector.tensor_copy(out=picked[i][:], in_=d_sb[i][:].indirect(p2[:]))
-            size[i] = ring.tile([P, NP], F32, name="size")
-            nc.scalar.activation(out=size[i][:], in_=picked[i][:], func=ACT.Abs)
+        def pick(i, c0, c1):
+            if c0 == 0:
+                picked[i] = ring.tile([P, NP], F32, name="picked")
+                size[i] = ring.tile([P, NP], F32, name="size")
+                gated[i] = ring.tile([P, NP], F32, name="gated")
+                result[i] = ring.tile([P, NP], F32, name="result")
+            nc.vector.tensor_copy(out=picked[i][:, c0:c1], in_=d_sb[i][:].indirect(p2[:, c0 // 16 : c1 // 16]))
+            nc.scalar.activation(out=size[i][:, c0:c1], in_=picked[i][:, c0:c1], func=ACT.Abs)
 
-        def pass_gate(i):
-            gated[i] = ring.tile([P, NP], F32, name="gated")
-            nc.vector.tensor_tensor(out=gated[i][:], in0=picked[i][:], in1=gate[i][:], op=ALU.mult)
+        def pass_gate(i, c0, c1):
+            nc.vector.tensor_tensor(out=gated[i][:, c0:c1], in0=picked[i][:, c0:c1], in1=gate[i][:, c0:c1], op=ALU.mult)
 
-        def finish(i):
-            result = ring.tile([P, NP], F32, name="result")
+        def finish(i, c0, c1):
             nc.vector.scalar_tensor_tensor(
-                out=result[:], in0=size[i][:], scalar=cols[:, 2 * ROW_TILES + i : 2 * ROW_TILES + i + 1],
-                in1=gated[i][:], op0=ALU.mult, op1=ALU.add,
+                out=result[i][:, c0:c1], in0=size[i][:, c0:c1],
+                scalar=cols[:, 2 * ROW_TILES + i : 2 * ROW_TILES + i + 1],
+                in1=gated[i][:, c0:c1], op0=ALU.mult, op1=ALU.add,
             )
-            nc.sync.dma_start(out=out[rows_of(i), :], in_=result[:])
+            nc.sync.dma_start(out=out[rows_of(i), c0:c1], in_=result[i][:, c0:c1])
 
-        for step in range(-1, ROW_TILES):
-            now, ahead = step >= 0, step + 1 < ROW_TILES
-            if now:
-                pick(step)
-            if ahead:
-                score_e(step + 1, 0)
-            if now:
-                pass_gate(step)
-            if ahead:
-                score_d(step + 1)
-                score_e(step + 1, 1)
-            if now:
-                finish(step)
-            if ahead:
-                look(step + 1)
+        result = {}
+        last = ROW_TILES - 1
+        score_e(0, 0)
+        for step in range(-1, last):
+            if step >= 0:
+                pick(step, 0, NP)
+            score_e(step + 1, 1)
+            make_bias(step + 1)
+            if step >= 0:
+                pass_gate(step, 0, NP)
+            if step + 2 <= last:
+                score_e(step + 2, 0)
+            score_d(step + 1)
+            if step >= 0:
+                finish(step, 0, NP)
+            look(step + 1)
+        parts = [(0, NP // 2), (NP // 2, NP)]
+        for stage in (pick, pass_gate, finish):
+            for c0, c1 in parts:
+                stage(last, c0, c1)

from contextlib import ExitStack

import concourse.mybir as mybir
from concourse.masks import make_identity

K, H, T, S, T3, S2, NP = 1024, 512, 4096, 1024, 2048, 1024, 512
FLOPS = 2 * (2 * K * H * S + 2 * H * S2 * S)

F32 = mybir.dt.float32
BF16 = mybir.dt.bfloat16
I32 = mybir.dt.int32
U32 = mybir.dt.uint32
U16 = mybir.dt.uint16
U8 = mybir.dt.uint8
FP8X4 = mybir.dt.float8_e4m3fn_x4
FP4X4 = mybir.dt.float4_e2m1fn_x4
ALU = mybir.AluOpType
ACT = mybir.ActivationFunctionType

P = 128
PACK = 4
BANK = 512
PASSES = K // (P * PACK)
HALVES = S // BANK
ROW_TILES = S2 // P
QUADS = 4
W3_LOADS = 2
W3_PIECE = 256


def tile_list_salt_screen_scores_kernel(
    tc, tab_words, tab_scales, offs, tab2_words, tab2_scales, offs2, pos1, pos2,
    w1, w2_words, w2_scales, gain, w3, steep, share, lat, out,
):
    nc = tc.nc
    with ExitStack() as ctx:
        keep = ctx.enter_context(tc.tile_pool(name="keep", bufs=1))
        ring = ctx.enter_context(tc.tile_pool(name="ring", bufs=3))
        turns = ctx.enter_context(tc.tile_pool(name="turns", bufs=1))
        psum = ctx.enter_context(tc.psum_pool(name="psum", bufs=1))

        def held(name, shape, dtype):
            return keep.tile(shape, dtype, name=name, align_bytes=64)

        def tenant(name, shape, dtype, kib):
            return turns.tile(shape, dtype, name=name, align_bytes=64, offset=int(kib * 1024))

        def bank(name, number):
            return psum.tile([P, BANK], F32, name=name, offset=number * BANK * 4)

        idx = held("idx", [P, S // 16], U16)
        idx2 = held("idx2", [P, S2 // 16], U16)
        p1 = held("p1", [P, NP // 16], U16)
        p2 = held("p2", [P, NP // 16], U16)

        tab_s = held("tab_s", [P, T], U8)
        tab2_s = held("tab2_s", [P, T3], U8)
        w2_s_raw = held("w2_s_raw", [P, PASSES * H], U8)
        v_planes = held("v_planes", [P, PASSES * S], U8)
        gain_t = held("gain_t", [P, PACK], F32)
        nc.vector.memset(w2_s_raw[:].bitcast(I32), 0)
        for q in range(QUADS):
            engine = nc.vector if q < QUADS // 2 else nc.gpsimd
            engine.memset(tab_s[:].bitcast(I32)[32 * q : 32 * q + 24, :], 0)
        nc.gpsimd.memset(tab2_s[:].bitcast(I32), 0)
        for q in range(QUADS):
            nc.gpsimd.dma_start(
                out=tab2_s[:].bitcast(I32)[32 * q : 32 * q + 4, :],
                in_=tab2_scales.bitcast(I32)[0, 4 * q : 4 * q + 4, :],
            )
        nc.vector.memset(v_planes[:].bitcast(I32)[96:128, :], 0)
        ident = held("ident", [P, P], F32)
        make_identity(nc, ident[:])

        tab_w = [tenant("tab_w0", [P, T], I32, 8)]
        w1_raw = [tenant("w1_raw%d" % a, [P, PACK, H], F32, 24 + 8 * a) for a in range(PASSES)]
        w2_raw = tenant("w2_raw", [P, PASSES, H], U16, 67)
        w3_cols = S2 // W3_LOADS

        def load_words(tile, words):
            nc.sync.dma_start(out=tile[:], in_=words.rearrange("p t i -> p (t i)").bitcast(I32))

        def load_w1(a):
            nc.sync.dma_start(out=w1_raw[a][:], in_=w1[a * 512 : (a + 1) * 512, :].rearrange("(p j) c -> p j c", j=PACK))

        for tile, source in ((idx, offs), (idx2, offs2), (p1, pos1)):
            nc.sync.dma_start(out=tile[:], in_=source)
        for q in range(QUADS):
            nc.sync.dma_start(
                out=tab_s[:].bitcast(I32)[32 * q + 24 : 32 * q + 32, :],
                in_=tab_scales.bitcast(I32)[:, 4 * q : 4 * q + 4, :],
            )
        load_words(tab_w[0], tab_words[0])
        nc.sync.dma_start(
            out=w2_raw[:].rearrange("p a c -> p (a c)").bitcast(I32).rearrange("p (a c) -> p a c", a=PASSES),
            in_=w2_words.bitcast(I32).rearrange("a p c -> p a c"),
        )
        load_w1(0)
        nc.sync.dma_start(out=p2[:], in_=pos2)
        nc.sync.dma_start(out=gain_t[:], in_=gain.rearrange("(p t) -> p t", t=PACK))
        load_w1(1)
        for q in range(QUADS):
            nc.scalar.dma_start(
                out=w2_s_raw[:].bitcast(I32)[32 * q : 32 * q + 4, :].rearrange("p (a c) -> p a c", a=PASSES),
                in_=w2_scales.bitcast(I32)[:, 4 * q : 4 * q + 4, :].rearrange("a r c -> r a c"),
            )

        v_s = held("v_s", [P, S], U8)
        nc.vector.tensor_copy(out=v_s[:], in_=tab_s[:].indirect(idx[:]))
        for a in range(PASSES):
            nc.sync.dma_start(
                out=v_planes[:, a * S : (a + 1) * S].bitcast(I32)[0:100, :],
                in_=v_s[:].bitcast(I32)[24 + 4 * a : 124 + 4 * a, :],
            )

        v_w = [
            [held("v_w0_%d" % hf, [P, BANK], U32) for hf in range(HALVES)],
            [tenant("v_w1_%d" % hf, [P, BANK], U32, 51 + 2 * hf) for hf in range(HALVES)],
        ]

        def gather_v(a, hf):
            nc.vector.tensor_copy(
                out=v_w[a][hf][:],
                in_=tab_w[a][:].bitcast(U32).indirect(idx[:, hf * 32 : (hf + 1) * 32]),
            )

        for hf in range(HALVES):
            gather_v(0, hf)
        tab_w.append(tenant("tab_w1", [P, T], I32, 0))
        load_words(tab_w[1], tab_words[1])

        w2_w = tenant("w2_w", [P, PASSES, H], U16, 16)
        for a in range(PASSES):
            nc.vector.tensor_copy(
                out=w2_w[:, a, :].rearrange("p (t m) -> p t m", t=PACK),
                in_=w2_raw[:, a, :].rearrange("p (m t) -> p t m", t=PACK),
            )


        w1_w = [tenant("w1_w%d" % a, [P, H], U32, 20 + 2 * a) for a in range(PASSES)]
        w1_s = [held("w1_s%d" % a, [P, H], U8) for a in range(PASSES)]
        for a in range(PASSES):
            w1_bf = tenant("w1_bf%d" % a, [P, H * PACK], BF16, 40 + 11 * a)
            nc.scalar.copy(
                out=w1_bf[:].rearrange("p (t m j) -> p m t j", t=PACK, j=PACK),
                in_=w1_raw[a][:].rearrange("p j (m t) -> p m t j", t=PACK),
            )
            nc.vector.quantize_mx(out=w1_w[a][:].bitcast(FP8X4), scales=w1_s[a][:], in_=w1_bf[:])
        tab2_w = tenant("tab2_w", [P, T3], I32, 67)
        load_words(tab2_w, tab2_words[0])
        w3_raw = []
        for b in range(W3_LOADS):
            w3_raw.append(tenant("w3_raw%d" % b, [P, PACK, w3_cols], F32, 43 - 10.5 * b))
            nc.sync.dma_start(
                out=w3_raw[b][:],
                in_=w3[:, b * w3_cols : (b + 1) * w3_cols].rearrange("(p j) c -> p j c", j=PACK),
            )


        w2_s = tenant("w2_s", [P, PASSES * H], U8, 40.5)
        nc.vector.tensor_copy(
            out=w2_s[:].rearrange("p (a t m) -> p a t m", a=PASSES, t=PACK),
            in_=w2_s_raw[:].rearrange("p (a m t) -> p a t m", a=PASSES, t=PACK),
        )
        rows = tenant("rows", [P, P], F32, 41.5)
        nc.vector.memset(rows[:], 0.0)
        for n, vec in enumerate((steep, share, lat)):
            nc.sync.dma_start(out=rows[ROW_TILES * n : ROW_TILES * (n + 1), :], in_=vec.rearrange("(i p) -> i p", p=P))
        v2_s = tenant("v2_s", [P, S2], U8, 42)
        nc.vector.tensor_copy(out=v2_s[:], in_=tab2_s[:].indirect(idx2[:]))
        for hf in range(HALVES):
            gather_v(1, hf)


        h_w = [held("h_w%d" % hf, [P, BANK], U32) for hf in range(HALVES)]
        h_s = [held("h_s%d" % hf, [P, BANK], U8) for hf in range(HALVES)]
        v2_w = tenant("v2_w", [P, S2], U32, 0)

        def v_scales(a, hf):
            return v_planes[:, a * S + hf * BANK : a * S + (hf + 1) * BANK]

        f_bank = {(hf, t): bank("f%d_%d" % (hf, t), PACK * hf + t) for hf in range(HALVES) for t in range(PACK)}
        bent = {}
        h_planes = [held("h_planes%d" % hf, [P, PACK, BANK], BF16) for hf in range(HALVES)]

        def f_pass(a, hf, t):
            nc.tensor.matmul_mx(
                out=f_bank[hf, t][:], lhsT=w1_w[a][:, t * P : (t + 1) * P].bitcast(FP8X4),
                lhsT_scale=w1_s[a][:, t * P : (t + 1) * P],
                rhs=v_w[a][hf][:].bitcast(FP8X4), rhs_scale=v_scales(a, hf),
                start=(a == 0), stop=(a == PASSES - 1),
            )

        def bend(hf, t):
            f_pass(1, hf, t)
            bent[hf, t] = tenant("bent%d_%d" % (hf, t), [P, BANK], F32, 76 + 2 * (PACK * hf + t))
            nc.scalar.activation(out=bent[hf, t][:], in_=f_bank[hf, t][:], func=ACT.Silu)

        def feature(hf, t):
            g_bank = bank("g%d_%d" % (hf, t), PACK * hf + t)
            for a in range(PASSES):
                nc.tensor.matmul_mx(
                    out=g_bank[:], lhsT=w2_w[:, a, t * P : (t + 1) * P].bitcast(FP4X4),
                    lhsT_scale=w2_s[:, a * H + t * P : a * H + (t + 1) * P],
                    rhs=v_w[a][hf][:].bitcast(FP8X4), rhs_scale=v_scales(a, hf),
                    start=(a == 0), stop=(a == PASSES - 1),
                )
            nc.vector.scalar_tensor_tensor(
                out=h_planes[hf][:, t, :], in0=bent[hf, t][:], scalar=gain_t[:, t : t + 1], in1=g_bank[:],
                op0=ALU.mult, op1=ALU.add,
            )

        def quantise_h(hf, weave):
            h_bf = tenant("h_bf%d" % hf, [P, BANK * PACK], BF16, 56 + 4 * hf)
            weave(
                out=h_bf[:].rearrange("p (c i t) -> p c t i", i=4, t=PACK),
                in_=h_planes[hf][:].rearrange("p t (c i) -> p c t i", i=4),
            )
            nc.vector.quantize_mx(out=h_w[hf][:].bitcast(FP8X4), scales=h_s[hf][:], in_=h_bf[:])

        def gather_v2(hf):
            nc.vector.tensor_copy(
                out=v2_w[:, hf * BANK : (hf + 1) * BANK],
                in_=tab2_w[:].bitcast(U32).indirect(idx2[:, hf * 32 : (hf + 1) * 32]),
            )

        for hf in range(HALVES):
            for t in range(PACK):
                f_pass(0, hf, t)
        for t in range(PACK):
            bend(0, t)
        for t in range(PACK):
            bend(1, t)
            feature(0, t)
        for t in range(PACK):
            feature(1, t)
        quantise_h(0, nc.scalar.copy)
        quantise_h(1, nc.vector.tensor_copy)
        for hf in range(HALVES):
            gather_v2(hf)

        turned = bank("turned", 7)
        nc.tensor.transpose(turned[:, :P], rows[:], ident[:])
        cols = held("cols", [P, 3 * ROW_TILES], F32)
        nc.scalar.copy(out=cols[:], in_=turned[:, : 3 * ROW_TILES])

        shift = held("shift", [P, ROW_TILES], F32)
        nc.vector.scalar_tensor_tensor(
            out=shift[:], in0=cols[:, :ROW_TILES], scalar=-1.0, in1=cols[:, ROW_TILES : 2 * ROW_TILES],
            op0=ALU.mult, op1=ALU.mult,
        )
        w3_w = tenant("w3_w", [P, S2], U32, 60)
        w3_s = held("w3_s", [P, S2], U8)

        def quantise_w3(piece):
            c0 = piece * W3_PIECE
            b, off = divmod(c0, w3_cols)
            if b == 0:
                w3_bf = held("w3_bf%d" % piece, [P, W3_PIECE * PACK], BF16)
                for c in range(0, W3_PIECE, P):
                    nc.gpsimd.tensor_scalar(
                        out=w3_bf[:, c * PACK : (c + P) * PACK].rearrange("p (c j) -> p c j", j=PACK),
                        in0=w3_raw[b][:, :, off + c : off + c + P].rearrange("p j c -> p c j"),
                        scalar1=1.0, scalar2=0.0, op0=ALU.mult, op1=ALU.add,
                    )
            else:
                w3_bf = tenant("w3_bf%d" % piece, [P, W3_PIECE * PACK], BF16, 78 + 2 * piece)
                nc.scalar.copy(
                    out=w3_bf[:].rearrange("p (c i j) -> p c j i", i=4, j=PACK),
                    in_=w3_raw[b][:, :, off : off + W3_PIECE].rearrange("p j (c i) -> p c j i", i=4),
                )
            nc.vector.quantize_mx(
                out=w3_w[:, c0 : c0 + W3_PIECE].bitcast(FP8X4), scales=w3_s[:, c0 : c0 + W3_PIECE], in_=w3_bf[:],
            )

        tops = held("tops", [P, HALVES * ROW_TILES], F32)
        bias = held("bias", [P, ROW_TILES], F32)
        e_sb, d_sb, gate, picked, size, gated = {}, {}, {}, {}, {}, {}

        def rows_of(i):
            return slice(i * P, (i + 1) * P)

        def score_e(i, hf):
            ms = rows_of(i)
            if hf == 0:
                e_sb[i] = ring.tile([P, S], F32, name="e_sb")
            e_bank = bank("e%d_%d" % (i, hf), 2 * (i % 2) + hf)
            nc.tensor.matmul_mx(
                out=e_bank[:], lhsT=v2_w[:, ms].bitcast(FP8X4), lhsT_scale=v2_s[:, ms],
                rhs=h_w[hf][:].bitcast(FP8X4), rhs_scale=h_s[hf][:], start=True, stop=True,
            )
            nc.vector.tensor_scalar(
                out=e_sb[i][:, hf * BANK : (hf + 1) * BANK], in0=e_bank[:], scalar1=1.0,
                scalar2=None if hf == 0 else tops[:, HALVES * i : HALVES * i + 1],
                op0=ALU.mult, op1=ALU.max, accum_out=tops[:, HALVES * i + hf : HALVES * i + hf + 1],
            )

        def score_d(i):
            ms = rows_of(i)
            if (i * P) % W3_PIECE == 0:
                quantise_w3(i * P // W3_PIECE)
            d_sb[i] = ring.tile([P, S], F32, name="d_sb")
            for hf in range(HALVES):
                d_bank = bank("d%d_%d" % (i, hf), 4 + 2 * (i % 2) + hf)
                nc.tensor.matmul_mx(
                    out=d_bank[:], lhsT=w3_w[:, ms].bitcast(FP8X4), lhsT_scale=w3_s[:, ms],
                    rhs=h_w[hf][:].bitcast(FP8X4), rhs_scale=h_s[hf][:], start=True, stop=True,
                )
                nc.scalar.copy(out=d_sb[i][:, hf * BANK : (hf + 1) * BANK], in_=d_bank[:])

        def make_bias(i):
            nc.scalar.activation(
                out=bias[:, i : i + 1], in_=tops[:, HALVES * i + 1 : HALVES * i + 2], func=ACT.Copy,
                scale=shift[:, i : i + 1],
            )

        def look(i):
            gate[i] = ring.tile([P, NP], F32, name="gate")
            nc.scalar.activation(
                out=gate[i][:], in_=e_sb[i][:].indirect(p1[:]), func=ACT.Sigmoid,
                bias=bias[:, i : i + 1], scale=cols[:, i : i + 1],
            )

        def pick(i, c0, c1):
            if c0 == 0:
                picked[i] = ring.tile([P, NP], F32, name="picked")
                size[i] = ring.tile([P, NP], F32, name="size")
                gated[i] = ring.tile([P, NP], F32, name="gated")
                result[i] = ring.tile([P, NP], F32, name="result")
            nc.vector.tensor_copy(out=picked[i][:, c0:c1], in_=d_sb[i][:].indirect(p2[:, c0 // 16 : c1 // 16]))
            nc.scalar.activation(out=size[i][:, c0:c1], in_=picked[i][:, c0:c1], func=ACT.Abs)

        def pass_gate(i, c0, c1):
            nc.vector.tensor_tensor(out=gated[i][:, c0:c1], in0=picked[i][:, c0:c1], in1=gate[i][:, c0:c1], op=ALU.mult)

        def finish(i, c0, c1):
            nc.vector.scalar_tensor_tensor(
                out=result[i][:, c0:c1], in0=size[i][:, c0:c1],
                scalar=cols[:, 2 * ROW_TILES + i : 2 * ROW_TILES + i + 1],
                in1=gated[i][:, c0:c1], op0=ALU.mult, op1=ALU.add,
            )
            nc.sync.dma_start(out=out[rows_of(i), c0:c1], in_=result[i][:, c0:c1])

        result = {}
        last = ROW_TILES - 1
        score_e(0, 0)
        for step in range(-1, last):
            if step >= 0:
                pick(step, 0, NP)
            score_e(step + 1, 1)
            make_bias(step + 1)
            if step >= 0:
                pass_gate(step, 0, NP)
            if step + 2 <= last:
                score_e(step + 2, 0)
            score_d(step + 1)
            if step >= 0:
                finish(step, 0, NP)
            look(step + 1)
        parts = [(0, NP // 2), (NP // 2, NP)]
        for stage in (pick, pass_gate, finish):
            for c0, c1 in parts:
                stage(last, c0, c1)
